import numpy as np
import ml_dtypes

BF16 = ml_dtypes.bfloat16


def bf(x):
    return np.asarray(x, np.float32).astype(BF16)


def f32(x):
    return np.asarray(x, np.float32)


def f64(x):
    return np.asarray(x).astype(np.float64)


def striped(idx):
    return np.tile(idx.reshape(-1, 16).T, (8, 1))


def rows(idx, k):
    return np.tile(idx, (k, 1))


def look(tab, idx):
    return np.take_along_axis(f64(tab), rows(idx, len(tab)), axis=1)


K, S, V, N, M = 128, 2048, 1024, 1024, 256


def angles():
    a = np.random.uniform(0.0, 2.0 * np.pi, (K, S))
    return np.stack([np.cos(a), np.sin(a)])


def setup_inputs():
    return {"tab": bf(angles()), "x0": bf(np.random.standard_normal((K, V))), "x1": bf(np.random.standard_normal((K, V))), "w": bf(np.random.standard_normal((K, M)) / np.sqrt(K)), "offs": striped(np.random.randint(0, S, N))}


def reference(tab, x0, x1, w, offs):
    idx = offs[:16].T.reshape(-1)
    x = f64(x0) * look(tab[0], idx) + f64(x1) * look(tab[1], idx)
    y = f64(w).T @ x
    return y

@@ -1,0 +1,52 @@
+import concourse.mybir as mybir
+
+BF16, F32, U16 = mybir.dt.bfloat16, mybir.dt.float32, mybir.dt.uint16
+MULT = mybir.AluOpType.mult
+
+P = 128
+PIECE = 512
+LANES = 16
+FLOPS = 2 * 128 * 256 * 1024 + 3 * 128 * 1024
+
+
+def tile_lookup_rope_mul_none_kernel(tc, tab, x0, x1, w, offs, out):
+    nc = tc.nc
+    S = tab.shape[2]
+    N = x0.shape[1]
+    M = w.shape[1]
+    pieces, blocks = N // PIECE, M // P
+
+    with (
+        tc.tile_pool(name="held", bufs=1) as held,
+        tc.psum_pool(name="psum", bufs=1) as psum,
+    ):
+        offsets = held.tile([P, N // LANES], U16, name="offsets")
+        cos = held.tile([P, S], BF16, name="cos")
+        sin = held.tile([P, S], BF16, name="sin")
+        x0_sb = held.tile([P, N], BF16, name="x0_sb")
+        x1_sb = held.tile([P, N], BF16, name="x1_sb")
+        w_sb = held.tile([P, M], BF16, name="w_sb")
+        nc.sync.dma_start(offsets[:], offs)
+        nc.sync.dma_start(cos[:], tab[0])
+        nc.sync.dma_start(x0_sb[:], x0)
+        nc.sync.dma_start(sin[:], tab[1])
+        nc.sync.dma_start(x1_sb[:], x1)
+        nc.sync.dma_start(w_sb[:], w)
+
+        banks = [[psum.tile([P, PIECE], F32, name=f"bank_{c}_{b}") for b in range(blocks)] for c in range(pieces)]
+
+        for term, (table, values) in enumerate(((cos, x0_sb), (sin, x1_sb))):
+            for c in range(pieces):
+                cols = slice(c * PIECE, (c + 1) * PIECE)
+                entries = offsets[:, c * PIECE // LANES : (c + 1) * PIECE // LANES]
+                product = held.tile([P, PIECE], BF16, name=f"product_{term}_{c}")
+                nc.vector.tensor_tensor(product[:], table[:].indirect(entries), values[:, cols], MULT)
+                for b in range(blocks):
+                    nc.tensor.matmul(banks[c][b][:], w_sb[:, b * P : (b + 1) * P], product[:],
+                                     start=(term == 0), stop=(term == 1))
+
+        for c in range(pieces):
+            for b in range(blocks):
+                staged = held.tile([P, PIECE], F32, name=f"staged_{c}_{b}")
+                nc.scalar.copy(staged[:], banks[c][b][:])
+                nc.sync.dma_start(out[b * P : (b + 1) * P, c * PIECE : (c + 1) * PIECE], staged[:])

@@ -5,6 +5,7 @@ MULT = mybir.AluOpType.mult
 
 P = 128
 PIECE = 512
+CHUNK = 256
 LANES = 16
 FLOPS = 2 * 128 * 256 * 1024 + 3 * 128 * 1024
 
@@ -14,7 +15,7 @@ def tile_lookup_rope_mul_none_kernel(tc, tab, x0, x1, w, offs, out):
     S = tab.shape[2]
     N = x0.shape[1]
     M = w.shape[1]
-    pieces, blocks = N // PIECE, M // P
+    pieces, chunks, blocks = N // PIECE, PIECE // CHUNK, M // P
 
     with (
         tc.tile_pool(name="held", bufs=1) as held,
@@ -26,27 +27,40 @@ def tile_lookup_rope_mul_none_kernel(tc, tab, x0, x1, w, offs, out):
         x0_sb = held.tile([P, N], BF16, name="x0_sb")
         x1_sb = held.tile([P, N], BF16, name="x1_sb")
         w_sb = held.tile([P, M], BF16, name="w_sb")
+        head, rest = slice(0, PIECE), slice(PIECE, N)
         nc.sync.dma_start(offsets[:], offs)
         nc.sync.dma_start(cos[:], tab[0])
-        nc.sync.dma_start(x0_sb[:], x0)
+        nc.sync.dma_start(x0_sb[:, head], x0[:, head])
         nc.sync.dma_start(sin[:], tab[1])
-        nc.sync.dma_start(x1_sb[:], x1)
+        nc.sync.dma_start(x1_sb[:, head], x1[:, head])
         nc.sync.dma_start(w_sb[:], w)
+        nc.sync.dma_start(x0_sb[:, rest], x0[:, rest])
+        nc.sync.dma_start(x1_sb[:, rest], x1[:, rest])
 
-        banks = [[psum.tile([P, PIECE], F32, name=f"bank_{c}_{b}") for b in range(blocks)] for c in range(pieces)]
-
-        for term, (table, values) in enumerate(((cos, x0_sb), (sin, x1_sb))):
-            for c in range(pieces):
-                cols = slice(c * PIECE, (c + 1) * PIECE)
-                entries = offsets[:, c * PIECE // LANES : (c + 1) * PIECE // LANES]
-                product = held.tile([P, PIECE], BF16, name=f"product_{term}_{c}")
-                nc.vector.tensor_tensor(product[:], table[:].indirect(entries), values[:, cols], MULT)
-                for b in range(blocks):
-                    nc.tensor.matmul(banks[c][b][:], w_sb[:, b * P : (b + 1) * P], product[:],
-                                     start=(term == 0), stop=(term == 1))
+        banks = {(c, b, h): psum.tile([P, CHUNK], F32, name=f"bank_{c}_{b}_{h}")
+                 for c in range(pieces) for b in range(blocks) for h in range(chunks)}
 
         for c in range(pieces):
+            entries = offsets[:, c * PIECE // LANES : (c + 1) * PIECE // LANES]
+            for term, (table, values) in enumerate(((cos, x0_sb), (sin, x1_sb))):
+                product = held.tile([P, PIECE], BF16, name=f"product_{term}_{c}")
+                nc.vector.tensor_tensor(product[:], table[:].indirect(entries),
+                                        values[:, c * PIECE : (c + 1) * PIECE], MULT)
+                for b in range(blocks):
+                    for h in range(chunks):
+                        nc.tensor.matmul(banks[c, b, h][:], w_sb[:, b * P : (b + 1) * P],
+                                         product[:, h * CHUNK : (h + 1) * CHUNK],
+                                         start=(term == 0), stop=(term == 1))
+
+        for c in range(pieces):
+            last = c == pieces - 1
             for b in range(blocks):
-                staged = held.tile([P, PIECE], F32, name=f"staged_{c}_{b}")
-                nc.scalar.copy(staged[:], banks[c][b][:])
-                nc.sync.dma_start(out[b * P : (b + 1) * P, c * PIECE : (c + 1) * PIECE], staged[:])
+                for h in range(chunks):
+                    staged = held.tile([P, CHUNK], F32, name=f"staged_{c}_{b}_{h}")
+                    if last and h % 2 == 0:
+                        nc.vector.tensor_copy(staged[:], banks[c, b, h][:])
+                    else:
+                        nc.scalar.copy(staged[:], banks[c, b, h][:])
+                    first = c * PIECE + h * CHUNK
+                    queue = nc.sync if last else nc.scalar
+                    queue.dma_start(out[b * P : (b + 1) * P, first : first + CHUNK], staged[:])

@@ -5,7 +5,7 @@ MULT = mybir.AluOpType.mult
 
 P = 128
 PIECE = 512
-CHUNK = 256
+TAIL_CHUNK = 256
 LANES = 16
 FLOPS = 2 * 128 * 256 * 1024 + 3 * 128 * 1024
 
@@ -15,7 +15,7 @@ def tile_lookup_rope_mul_none_kernel(tc, tab, x0, x1, w, offs, out):
     S = tab.shape[2]
     N = x0.shape[1]
     M = w.shape[1]
-    pieces, chunks, blocks = N // PIECE, PIECE // CHUNK, M // P
+    pieces, blocks = N // PIECE, M // P
 
     with (
         tc.tile_pool(name="held", bufs=1) as held,
@@ -37,30 +37,28 @@ def tile_lookup_rope_mul_none_kernel(tc, tab, x0, x1, w, offs, out):
         nc.sync.dma_start(x0_sb[:, rest], x0[:, rest])
         nc.sync.dma_start(x1_sb[:, rest], x1[:, rest])
 
-        banks = {(c, b, h): psum.tile([P, CHUNK], F32, name=f"bank_{c}_{b}_{h}")
-                 for c in range(pieces) for b in range(blocks) for h in range(chunks)}
-
         for c in range(pieces):
+            last = c == pieces - 1
+            width = TAIL_CHUNK if last else PIECE
+            chunks = [(b, h) for b in range(blocks) for h in range(PIECE // width)]
+            banks = {(b, h): psum.tile([P, width], F32, name=f"bank_{c}_{b}_{h}") for b, h in chunks}
             entries = offsets[:, c * PIECE // LANES : (c + 1) * PIECE // LANES]
+
             for term, (table, values) in enumerate(((cos, x0_sb), (sin, x1_sb))):
                 product = held.tile([P, PIECE], BF16, name=f"product_{term}_{c}")
                 nc.vector.tensor_tensor(product[:], table[:].indirect(entries),
                                         values[:, c * PIECE : (c + 1) * PIECE], MULT)
-                for b in range(blocks):
-                    for h in range(chunks):
-                        nc.tensor.matmul(banks[c, b, h][:], w_sb[:, b * P : (b + 1) * P],
-                                         product[:, h * CHUNK : (h + 1) * CHUNK],
-                                         start=(term == 0), stop=(term == 1))
+                for b, h in chunks:
+                    nc.tensor.matmul(banks[b, h][:], w_sb[:, b * P : (b + 1) * P],
+                                     product[:, h * width : (h + 1) * width],
+                                     start=(term == 0), stop=(term == 1))
 
-        for c in range(pieces):
-            last = c == pieces - 1
-            for b in range(blocks):
-                for h in range(chunks):
-                    staged = held.tile([P, CHUNK], F32, name=f"staged_{c}_{b}_{h}")
-                    if last and h % 2 == 0:
-                        nc.vector.tensor_copy(staged[:], banks[c, b, h][:])
-                    else:
-                        nc.scalar.copy(staged[:], banks[c, b, h][:])
-                    first = c * PIECE + h * CHUNK
-                    queue = nc.sync if last else nc.scalar
-                    queue.dma_start(out[b * P : (b + 1) * P, first : first + CHUNK], staged[:])
+            for b, h in chunks:
+                staged = held.tile([P, width], F32, name=f"staged_{c}_{b}_{h}")
+                if last and h % 2 == 0:
+                    nc.vector.tensor_copy(staged[:], banks[b, h][:])
+                else:
+                    nc.scalar.copy(staged[:], banks[b, h][:])
+                first = c * PIECE + h * width
+                queue = nc.sync if last else nc.scalar
+                queue.dma_start(out[b * P : (b + 1) * P, first : first + width], staged[:])

import concourse.mybir as mybir

BF16, F32, U16 = mybir.dt.bfloat16, mybir.dt.float32, mybir.dt.uint16
MULT = mybir.AluOpType.mult

P = 128
PIECE = 512
TAIL_CHUNK = 256
LANES = 16
FLOPS = 2 * 128 * 256 * 1024 + 3 * 128 * 1024


def tile_lookup_rope_mul_none_kernel(tc, tab, x0, x1, w, offs, out):
    nc = tc.nc
    S = tab.shape[2]
    N = x0.shape[1]
    M = w.shape[1]
    pieces, blocks = N // PIECE, M // P

    with (
        tc.tile_pool(name="held", bufs=1) as held,
        tc.psum_pool(name="psum", bufs=1) as psum,
    ):
        offsets = held.tile([P, N // LANES], U16, name="offsets")
        cos = held.tile([P, S], BF16, name="cos")
        sin = held.tile([P, S], BF16, name="sin")
        x0_sb = held.tile([P, N], BF16, name="x0_sb")
        x1_sb = held.tile([P, N], BF16, name="x1_sb")
        w_sb = held.tile([P, M], BF16, name="w_sb")
        head, rest = slice(0, PIECE), slice(PIECE, N)
        nc.sync.dma_start(offsets[:], offs)
        nc.sync.dma_start(cos[:], tab[0])
        nc.sync.dma_start(x0_sb[:, head], x0[:, head])
        nc.sync.dma_start(sin[:], tab[1])
        nc.sync.dma_start(x1_sb[:, head], x1[:, head])
        nc.sync.dma_start(w_sb[:], w)
        nc.sync.dma_start(x0_sb[:, rest], x0[:, rest])
        nc.sync.dma_start(x1_sb[:, rest], x1[:, rest])

        for c in range(pieces):
            last = c == pieces - 1
            width = TAIL_CHUNK if last else PIECE
            chunks = [(b, h) for b in range(blocks) for h in range(PIECE // width)]
            banks = {(b, h): psum.tile([P, width], F32, name=f"bank_{c}_{b}_{h}") for b, h in chunks}
            entries = offsets[:, c * PIECE // LANES : (c + 1) * PIECE // LANES]

            for term, (table, values) in enumerate(((cos, x0_sb), (sin, x1_sb))):
                product = held.tile([P, PIECE], BF16, name=f"product_{term}_{c}")
                nc.vector.tensor_tensor(product[:], table[:].indirect(entries),
                                        values[:, c * PIECE : (c + 1) * PIECE], MULT)
                for b, h in chunks:
                    nc.tensor.matmul(banks[b, h][:], w_sb[:, b * P : (b + 1) * P],
                                     product[:, h * width : (h + 1) * width],
                                     start=(term == 0), stop=(term == 1))

            for b, h in chunks:
                staged = held.tile([P, width], F32, name=f"staged_{c}_{b}_{h}")
                if last and h % 2 == 0:
                    nc.vector.tensor_copy(staged[:], banks[b, h][:])
                else:
                    nc.scalar.copy(staged[:], banks[b, h][:])
                first = c * PIECE + h * width
                queue = nc.sync if last else nc.scalar
                queue.dma_start(out[b * P : (b + 1) * P, first : first + width], staged[:])
